import numpy as np
import ml_dtypes


def mxq(x, axis, fmt="e4m3"):
    dtype, down = {"e4m3": (ml_dtypes.float8_e4m3fn, 7), "e5m2": (ml_dtypes.float8_e5m2, 14)}[fmt]
    v = np.moveaxis(np.asarray(x, np.float32).astype(ml_dtypes.bfloat16).astype(np.float64), axis, -1)
    blocks = v.reshape(v.shape[:-1] + (-1, 32))
    amax = np.abs(blocks).max(-1, keepdims=True)
    byte = np.maximum(np.where(amax > 0, np.frexp(amax)[1] - 1 + 127, 0) - down, 1)
    scale = np.exp2(byte - 127.0)
    codes = (blocks / scale).astype(np.float32).astype(dtype).astype(np.float64)
    return np.moveaxis((codes * scale).reshape(v.shape), -1, axis)


WIDE = False


def mx_kscale(k):
    if not WIDE:
        return np.ones(k)
    levels = np.array([10, -10, 5, -5, 0])
    if k % 512:
        return np.exp2(np.random.permutation(np.resize(levels, k // 32))).repeat(32)
    a = np.empty((k // 512, 16))
    for p in range(k // 512):
        a[p, :8] = np.random.permutation(np.resize(levels, 8))
        for g in range(8):
            far = levels[np.abs(levels - a[p, g]) >= 10]
            a[p, g + 8] = far[np.random.randint(len(far))]
    return np.exp2(a.ravel()).repeat(32)


BF16 = ml_dtypes.bfloat16


def bf(x):
    return np.asarray(x, np.float32).astype(BF16)


def f64(x):
    return np.asarray(x).astype(np.float64)


E2M1 = np.array([0.0, 0.5, 1.0, 1.5, 2.0, 3.0, 4.0, 6.0, -0.0, -0.5, -1.0, -1.5, -2.0, -3.0, -4.0, -6.0])


def pack_weight(w, fmt):
    k, n = w.shape
    w = f64(bf(w)).reshape(k // 32, 32, n)
    amax = np.abs(w).max(1)
    if fmt == "e4m3":
        byte = np.frexp(amax)[1] - 1 + 127 - 7
    else:
        mant, ex = np.frexp(amax / 6.0)
        byte = np.where(mant > 0.5, ex, ex - 1) + 127
    byte = np.clip(np.where(amax > 0, byte, 1), 1, 254)
    scaled = (w * np.exp2(127.0 - byte)[:, None, :]).reshape(k, n).astype(np.float32)
    by_word = np.ascontiguousarray(scaled.reshape(k // 512, 128, 4, n).transpose(0, 1, 3, 2))
    if fmt == "e4m3":
        words = by_word.astype(ml_dtypes.float8_e4m3fn).view(np.uint8)
    else:
        c = by_word.astype(ml_dtypes.float4_e2m1fn).view(np.uint8) & 0xF
        words = c[..., 0::2] | (c[..., 1::2] << 4)
    return np.ascontiguousarray(words), np.ascontiguousarray(byte.astype(np.uint8).reshape(k // 512, 16, n))


def unpack_weight(words, scales, fmt):
    g, p, n, _ = words.shape
    if fmt == "e4m3":
        vals = np.ascontiguousarray(words).view(ml_dtypes.float8_e4m3fn).astype(np.float64)
    else:
        nib = np.empty((g, p, n, 4), np.uint8)
        nib[..., 0::2] = words & 0xF
        nib[..., 1::2] = words >> 4
        vals = E2M1[nib]
    vals = vals * np.repeat(np.exp2(scales.astype(np.float64) - 127.0), 8, axis=1)[..., None]
    return vals.transpose(0, 1, 3, 2).reshape(g * 512, n)
def pack4(w):
    words, scales = pack_weight(w, "e2m1")
    return words.reshape(words.shape[0], 128, -1), scales


def unpack4(words, scales):
    return unpack_weight(words.reshape(words.shape[0], 128, -1, 2), scales, "e2m1")


def planes(Y):
    n, m = Y.shape
    b = f64(bf(Y)).reshape(n // 32, 32, m)
    amax = np.abs(b).max(1)
    byte = np.clip(np.where(amax > 0, np.frexp(amax)[1] - 1 + 127 - 7, 1), 1, 254)
    codes = (b * np.exp2(127.0 - byte)[:, None, :]).reshape(n, m).astype(np.float32).astype(ml_dtypes.float8_e4m3fn).view(np.uint8)
    words = codes.reshape(n // 512, 128, 4, m).transpose(0, 1, 3, 2)
    return np.ascontiguousarray(words), np.ascontiguousarray(byte.astype(np.uint8).reshape(n // 512, 16, m))


I, S, J, K, M = 1536, 1024, 1024, 512, 1024

def setup_inputs():
    rn = np.random.randn
    a = mx_kscale(S)
    b = mx_kscale(K)
    c = mx_kscale(J)
    expo = rn(S, I) * a[:, None]
    migr = rn(S, J) / (S ** 0.5 * J ** 0.25) / a[:, None]
    expo_words, expo_scales = pack_weight(f64(bf(expo)), "e4m3")
    migr_words, migr_scales = pack4(f64(bf(migr)))
    return {
        "expo_words": expo_words, "expo_scales": expo_scales,
        "migr_words": migr_words, "migr_scales": migr_scales,
        "stress": bf(np.exp(0.3 * rn(J)) * c),
        "loadings": bf(rn(J, K) / J ** 0.25 * b[None, :] / c[:, None]),
        "factors": bf(rn(K, M) / K ** 0.5 / b[:, None]),
        "base": bf(0.5 * rn(J) / J ** 0.25 / c),
        "duration": bf(1 + 0.1 * rn(I)),
        "convexity": bf(0.2 * np.exp(0.3 * rn(I))),
        "notional": bf(np.exp(0.8 * rn(I))),
    }

def reference(expo_words, expo_scales, migr_words, migr_scales, stress, loadings, factors, base, duration, convexity, notional):
    E = unpack_weight(expo_words, expo_scales, "e4m3")
    T = unpack4(migr_words, migr_scales)
    H = (E.T @ T) * f64(stress)[None, :]
    R = (mxq(f64(loadings), 1, "e4m3") @ mxq(f64(factors), 0, "e4m3")) + f64(base)[:, None]
    v = mxq(H, 1, "e4m3") @ mxq(R, 0, "e4m3")
    y = f64(notional)[:, None] * (v * (f64(convexity)[:, None] * v - f64(duration)[:, None]))
    Y = y
    words, scales = planes(Y)
    return y, words, scales

@@ -1,0 +1,338 @@
+from contextlib import ExitStack
+
+import concourse.mybir as mybir
+from concourse.masks import make_identity
+
+I, S, J, K, M = 1536, 1024, 1024, 512, 1024
+FLOPS = 2 * I * S * J + 2 * J * K * M + 2 * I * J * M
+
+F32 = mybir.dt.float32
+BF16 = mybir.dt.bfloat16
+I32 = mybir.dt.int32
+U32 = mybir.dt.uint32
+U8 = mybir.dt.uint8
+FP8X4 = mybir.dt.float8_e4m3fn_x4
+FP4X4 = mybir.dt.float4_e2m1fn_x4
+ALU = mybir.AluOpType
+ACT = mybir.ActivationFunctionType
+
+P = 128
+T4 = 4
+W = 512
+BANKS = 8
+
+RING = {"flat": 4, "woven": 8, "y": 6, "slope": 4}
+LOADS = "L1 T E0 F0 L0 F1 E2 E1"
+ORDER = """
+fw104p pm0 tr10 pm1 tr11 vec ha010 lq1 fw004v ha000 ha011 tr00 tr01 ha012 ha001 fq0 lq0 ha210 ha013 ha002 ivec
+fq1 rd010 hw0134a rd000 ha003 ha211 hw0103v rd001 ra110 rd002 ha212 rd011 ra111 rd100 rd012 ra112 hq01 hw0004p
+rd013 ra113 ha213 rw1104p hw2114a rd101 hw2101a rd003 rd102 rd103 ha100 hd110 ha101 ha200 ha102 rq01 ha103
+ha201 hw1024a rq00 hq21 rq11 hq00 ha202 rq10 hd111 hd112 hw1002p hd113 ha203 hq10 hq11 v000 v001 v010 v002
+hw2004p v003 hq20 v100 yw0004p v101 v102 v103 v011 v210 v211 v012 v013 v110 v111 v212 v213 yq00 v200 v201 v202
+v112 v113 yw1004p yw0102p yw2104p v203 yq10 yq21 yw0124a yq01 yw1104a yw2034a yw2003v yq11 yq20
+"""
+
+
+def tile_migration_spread_revaluation_k4_kernel(
+    tc, expo_words, expo_scales, migr_words, migr_scales, stress, loadings, factors, base,
+    duration, convexity, notional, out_0, out_1, out_2,
+):
+    nc = tc.nc
+    with ExitStack() as ctx:
+        keep = ctx.enter_context(tc.tile_pool(name="keep", bufs=1))
+        work = ctx.enter_context(tc.tile_pool(name="work", bufs=1))
+        psum = ctx.enter_context(tc.psum_pool(name="psum", bufs=1))
+        ctx.enter_context(tc.manual_schedule())
+
+        def kept(name, shape, dtype):
+            return keep.tile(shape, dtype, name=name, align_bytes=64)
+
+        tiles = {}
+        finished = []
+        bank_count = []
+
+        def bank(dtype, cols):
+            tag = "bank%d" % (len(bank_count) % BANKS)
+            bank_count.append(0)
+            return psum.tile([P, cols], dtype, name=tag, tag=tag)
+
+        t_raw = kept("t_raw", [P, 2, 2 * J], U8)
+        ts_raw = kept("ts_raw", [P, 2, J], U8)
+        t_words = kept("t_words", [P, 2, 2 * J], U8)
+        t_scales = kept("t_scales", [P, 2, J], U8)
+        e_words = [kept("e_words%d" % G, [P, 2, W], U32) for G in range(3)]
+        e_scales = kept("e_scales", [P, 2, I], U8)
+        l_raw = [kept("l_raw%d" % g, [P, T4, K], BF16) for g in range(2)]
+        l_codes = kept("l_codes", [P, 2, W], U32)
+        l_scales = kept("l_scales", [P, 2, W], U8)
+        f_raw = [kept("f_raw%d" % h, [P, T4, W], BF16) for h in range(2)]
+        f_codes = kept("f_codes", [P, 2, W], U32)
+        f_scales = kept("f_scales", [P, 2, W], U8)
+        h_codes = kept("h_codes", [P, 3, 2, W], U32)
+        h_scales = kept("h_scales", [P, 3, 2, W], U8)
+        r_codes = kept("r_codes", [P, 2, 2, W], U32)
+        r_scales = kept("r_scales", [P, 2, 2, W], U8)
+        y_codes = kept("y_codes", [P, 3, M], U32)
+        y_scales = kept("y_scales", [P, 3, M], U8)
+        rows = kept("rows", [P, 2 * P], BF16)
+        per_j = kept("per_j", [P, 2, 2 * T4], F32)
+        dur = kept("dur", [P, 3, T4], BF16)
+        cvx = kept("cvx", [P, 3, T4], BF16)
+        ntl = kept("ntl", [P, 3, T4], BF16)
+        quad = kept("quad", [P, 3, T4], F32)
+        lin = kept("lin", [P, 3, T4], F32)
+        ident = kept("ident", [P, P], F32)
+        ident16 = kept("ident16", [P, P], BF16)
+        warm = kept("warm", [P, 1], F32)
+
+        nc.vector.memset(ts_raw[:].rearrange("p s n -> p (s n)").bitcast(I32), 0)
+        nc.vector.memset(rows[:], 0.0)
+        nc.vector.memset(e_scales[:].rearrange("p s n -> p (s n)").bitcast(I32), 0)
+        make_identity(nc, ident[:])
+
+        def load_scales(queue, plane, src):
+            for Q in range(4):
+                queue.dma_start(
+                    out=plane[32 * Q : 32 * Q + 4].bitcast(I32),
+                    in_=src[:, 4 * Q : 4 * Q + 4, :].rearrange("s r n -> r s n").bitcast(I32),
+                )
+
+        def load_e(G):
+            nc.sync.dma_start(
+                out=e_words[G][:].bitcast(I32),
+                in_=expo_words[:, :, W * G : W * (G + 1), :].rearrange("s p n t -> p s (n t)").bitcast(I32),
+            )
+
+        def load_l(g):
+            nc.sync.dma_start(out=l_raw[g][:], in_=loadings[W * g : W * (g + 1), :].rearrange("(p e) k -> p e k", e=T4))
+
+        def load_f(h):
+            nc.sync.dma_start(out=f_raw[h][:], in_=factors[:, W * h : W * (h + 1)].rearrange("(p t) m -> p t m", t=T4))
+
+        def load_t():
+            nc.sync.dma_start(out=t_raw[:].bitcast(I32), in_=migr_words.rearrange("s p n -> p s n").bitcast(I32))
+
+        for n, vec in enumerate((stress, base)):
+            nc.gpsimd.dma_start(
+                out=rows[T4 * n : T4 * (n + 1), :].rearrange("t (c e) -> t c e", e=T4),
+                in_=vec.rearrange("(c t e) -> t c e", t=T4, e=T4),
+            )
+        make_identity(nc, ident16[:])
+        load_scales(nc.scalar, ts_raw, migr_scales)
+        nc.scalar.activation(out=warm[:], in_=ident[:, 0:1], func=ACT.Identity)
+        for n, name in enumerate(LOADS.split()):
+            if n == 4:
+                load_scales(nc.scalar, e_scales, expo_scales)
+            if n == 6:
+                for tile, vec in ((dur, duration), (cvx, convexity), (ntl, notional)):
+                    nc.sync.dma_start(out=tile[:], in_=vec.rearrange("(G p t) -> p G t", p=P, t=T4))
+            if name == "T":
+                load_t()
+            else:
+                {"L": load_l, "F": load_f, "E": load_e}[name[0]](int(name[1]))
+
+        def permute_t(g):
+            nc.vector.tensor_copy(
+                out=t_words[:, :, 2 * W * g : 2 * W * (g + 1)].bitcast(I32).rearrange("p s (t c w) -> p s t c w", t=T4, w=2),
+                in_=t_raw[:, :, 2 * W * g : 2 * W * (g + 1)].bitcast(I32).rearrange("p s (c t w) -> p s t c w", t=T4, w=2),
+            )
+            nc.vector.tensor_copy(
+                out=t_scales[:, :, W * g : W * (g + 1)].bitcast(I32).rearrange("p s (t c) -> p s t c", t=T4),
+                in_=ts_raw[:, :, W * g : W * (g + 1)].bitcast(I32).rearrange("p s (c t) -> p s t c", t=T4),
+            )
+
+        def turn_vectors():
+            b = bank(BF16, 2 * P)
+            for g in range(2):
+                nc.tensor.transpose(b[:, P * g : P * (g + 1)], rows[:, P * g : P * (g + 1)], ident16[:])
+            nc.vector.tensor_copy(out=per_j[:], in_=b[:].rearrange("p (g x) -> p g x", g=2)[:, :, 0 : 2 * T4])
+
+        def issuer_vectors():
+            nc.vector.tensor_tensor(out=quad[:], in0=ntl[:], in1=cvx[:], op=ALU.mult)
+            nc.vector.scalar_tensor_tensor(out=lin[:], in0=ntl[:], scalar=-1.0, in1=dur[:], op0=ALU.mult, op1=ALU.mult)
+
+        def turn_l(g, half):
+            b = bank(F32, W)
+            words = l_raw[g][:].bitcast(F32)
+            for x in range(2):
+                for u in range(2):
+                    n = 2 * x + u
+                    nc.tensor.transpose(b[:, P * n : P * (n + 1)], words[:, 2 * half + x, u : K // 2 : 2], ident[:])
+            dst = stage("l_woven", g)[:].rearrange("p n t -> p (n t)").bitcast(F32)
+            nc.scalar.copy(
+                out=dst.rearrange("p (t c h n) -> p t c h n", t=T4, h=2, n=4)[:, :, :, half, :],
+                in_=b[:].rearrange("p (n c t) -> p t c n", n=4, t=T4),
+            )
+
+        def weave(engine, dst, src, q0, q1):
+            out = dst[:, P * q0 : P * q1, :].rearrange("p (c i) t -> p c t i", i=4)
+            in_ = src[:, :, P * q0 : P * q1].rearrange("p t (c i) -> p c t i", i=4)
+            if engine == "v":
+                nc.vector.tensor_copy(out=out, in_=in_)
+            elif engine == "a":
+                nc.scalar.copy(out=out, in_=in_)
+            else:
+                nc.gpsimd.tensor_scalar(out=out, in0=in_, scalar1=1.0, scalar2=1.0, op0=ALU.mult, op1=ALU.mult)
+
+        def quantize(codes, scales, woven):
+            nc.vector.quantize_mx(out=codes.bitcast(FP8X4), scales=scales, in_=woven.rearrange("p n t -> p (n t)"))
+
+
+        used = {"flat": 0, "woven": 0, "y": 0, "slope": 0}
+
+        def fresh(ring, shape, dtype):
+            tag = "%s%d" % (ring, used[ring] % RING[ring])
+            used[ring] = used[ring] + 1
+            return work.tile(shape, dtype, name=tag, tag=tag, align_bytes=64)
+
+        def stage(kind, key):
+            if (kind, key) not in tiles:
+                ring = kind.split("_")[-1]
+                shape = [P, W, T4] if ring == "woven" else [P, T4, W]
+                tiles[(kind, key)] = fresh(ring, shape, F32 if ring == "y" else BF16)
+            return tiles[(kind, key)]
+
+        def h_matmul(out, G, g, t, n0, n1):
+            col = W * g + P * t
+            for s in range(2):
+                nc.tensor.matmul_mx(
+                    out=out,
+                    lhsT=t_words[:, s, 2 * col : 2 * (col + P)].bitcast(FP4X4),
+                    lhsT_scale=t_scales[:, s, col : col + P],
+                    rhs=e_words[G][:, s, n0:n1].bitcast(FP8X4),
+                    rhs_scale=e_scales[:, s, W * G + n0 : W * G + n1],
+                    start=(s == 0),
+                    stop=(s == 1),
+                )
+
+        def h_act(G, g, t):
+            b = bank(F32, W)
+            h_matmul(b[:], G, g, t, 0, W)
+            flat = stage("h_flat", (G, g))
+            nc.scalar.activation(
+                out=flat[:, t, :].rearrange("p (u q) -> p u q", u=T4),
+                in_=b[:].rearrange("p (q u) -> p u q", u=T4),
+                func=ACT.Copy,
+                scale=per_j[:, g, t : t + 1],
+            )
+
+        def h_dve(G, g, c):
+            b = bank(F32, W)
+            for t in range(T4):
+                h_matmul(b[:, P * t : P * (t + 1)], G, g, t, P * c, P * (c + 1))
+            woven = stage("h_woven", (G, g))
+            nc.vector.tensor_tensor(
+                out=woven[:].rearrange("p (u q) t -> p u q t", u=T4)[:, :, 32 * c : 32 * (c + 1), :],
+                in0=b[:].rearrange("p (t q u) -> p u q t", t=T4, u=T4),
+                in1=per_j[:, g, 0:T4].unsqueeze(1).unsqueeze(1).to_broadcast([P, T4, 32, T4]),
+                op=ALU.mult,
+            )
+
+        def r_matmul(out, h, g, t, n0, n1):
+            nc.tensor.matmul_mx(
+                out=out,
+                lhsT=l_codes[:, g, P * t : P * (t + 1)].bitcast(FP8X4),
+                lhsT_scale=l_scales[:, g, P * t : P * (t + 1)],
+                rhs=f_codes[:, h, n0:n1].bitcast(FP8X4),
+                rhs_scale=f_scales[:, h, n0:n1],
+                start=True,
+                stop=True,
+            )
+
+        def r_dve(h, g, c):
+            b = bank(F32, W)
+            for t in range(T4):
+                r_matmul(b[:, P * t : P * (t + 1)], h, g, t, P * c, P * (c + 1))
+            woven = stage("r_woven", (h, g))
+            nc.vector.tensor_tensor(
+                out=woven[:, P * c : P * (c + 1), :],
+                in0=b[:].rearrange("p (t n) -> p n t", t=T4),
+                in1=per_j[:, g, T4 : 2 * T4].unsqueeze(1).to_broadcast([P, P, T4]),
+                op=ALU.add,
+            )
+
+        def r_act(h, g, t):
+            b = bank(F32, W)
+            r_matmul(b[:], h, g, t, 0, W)
+            flat = stage("r_flat", (h, g))
+            nc.scalar.activation(out=flat[:, t, :], in_=b[:], func=ACT.Identity, bias=per_j[:, g, T4 + t : T4 + t + 1])
+
+        def value(G, h, t):
+            b = bank(F32, W)
+            for g in range(2):
+                nc.tensor.matmul_mx(
+                    out=b[:],
+                    lhsT=h_codes[:, G, g, P * t : P * (t + 1)].bitcast(FP8X4),
+                    lhsT_scale=h_scales[:, G, g, P * t : P * (t + 1)],
+                    rhs=r_codes[:, h, g, :].bitcast(FP8X4),
+                    rhs_scale=r_scales[:, h, g, :],
+                    start=(g == 0),
+                    stop=(g == 1),
+                )
+            slope = fresh("slope", [P, W], F32)
+            nc.scalar.activation(
+                out=slope[:], in_=b[:], func=ACT.Identity, scale=quad[:, G, t : t + 1], bias=lin[:, G, t : t + 1]
+            )
+            y = stage("y", (G, h))
+            nc.vector.tensor_tensor(out=y[:, t, :], in0=b[:], in1=slope[:], op=ALU.mult)
+            nc.sync.dma_start(
+                out=out_0[W * G : W * (G + 1), W * h : W * (h + 1)].rearrange("(p t) m -> p t m", t=T4)[:, t, :],
+                in_=y[:, t, :],
+            )
+
+        def y_planes(G, h):
+            cols = slice(W * h, W * (h + 1))
+            quantize(y_codes[:, G, cols], y_scales[:, G, cols], tiles[("y_woven", (G, h))][:])
+            nc.sync.dma_start(
+                out=out_1[G, :, cols, :].rearrange("p m t -> p (m t)").bitcast(I32), in_=y_codes[:, G, cols].bitcast(I32)
+            )
+            finished.append(G)
+            if len([x for x in finished if x == G]) == 2:
+                groups = slice(G, G + 1)
+                for Q in range(4):
+                    nc.sync.dma_start(
+                        out=out_2[groups, 4 * Q : 4 * Q + 4, :].rearrange("G r m -> r G m").bitcast(I32),
+                        in_=y_scales[32 * Q : 32 * Q + 4, groups, :].bitcast(I32),
+                    )
+
+        for step in ORDER.split():
+            kind, d = step[:2], [int(ch) for ch in step if ch in "0123456789"]
+            if kind == "pm":
+                permute_t(d[0])
+            elif step == "vec":
+                turn_vectors()
+            elif step == "ivec":
+                issuer_vectors()
+            elif kind == "tr":
+                turn_l(d[0], d[1])
+            elif kind == "lq":
+                quantize(l_codes[:, d[0], :], l_scales[:, d[0], :], stage("l_woven", d[0])[:])
+            elif kind == "fw":
+                weave(step[-1], stage("f_woven", d[0]), f_raw[d[0]], d[1], d[2])
+            elif kind == "fq":
+                quantize(f_codes[:, d[0], :], f_scales[:, d[0], :], stage("f_woven", d[0])[:])
+            elif kind == "ha":
+                h_act(d[0], d[1], d[2])
+            elif kind == "hd":
+                h_dve(d[0], d[1], d[2])
+            elif kind == "hw":
+                key = (d[0], d[1])
+                weave(step[-1], stage("h_woven", key), tiles[("h_flat", key)], d[2], d[3])
+            elif kind == "hq":
+                quantize(h_codes[:, d[0], d[1], :], h_scales[:, d[0], d[1], :], tiles[("h_woven", (d[0], d[1]))][:])
+            elif kind == "rd":
+                r_dve(d[0], d[1], d[2])
+            elif kind == "ra":
+                r_act(d[0], d[1], d[2])
+            elif kind == "rw":
+                key = (d[0], d[1])
+                weave(step[-1], stage("r_woven", key), tiles[("r_flat", key)], d[2], d[3])
+            elif kind == "rq":
+                quantize(r_codes[:, d[0], d[1], :], r_scales[:, d[0], d[1], :], tiles[("r_woven", (d[0], d[1]))][:])
+            elif kind == "yw":
+                key = (d[0], d[1])
+                weave(step[-1], stage("y_woven", key), tiles[("y", key)], d[2], d[3])
+            elif kind == "yq":
+                y_planes(d[0], d[1])
+            else:
+                value(d[0], d[1], d[2])

@@ -22,14 +22,15 @@ W = 512
 BANKS = 8
 
 RING = {"flat": 4, "woven": 8, "y": 6, "slope": 4}
-LOADS = "L1 T E0 F0 L0 F1 E2 E1"
+LOADS = "L0 F0 L1 Ts F1 E0 T0 T1 E2 Es E1"
 ORDER = """
-fw104p pm0 tr10 pm1 tr11 vec ha010 lq1 fw004v ha000 ha011 tr00 tr01 ha012 ha001 fq0 lq0 ha210 ha013 ha002 ivec
-fq1 rd010 hw0134a rd000 ha003 ha211 hw0103v rd001 ra110 rd002 ha212 rd011 ra111 rd100 rd012 ra112 hq01 hw0004p
-rd013 ra113 ha213 rw1104p hw2114a rd101 hw2101a rd003 rd102 rd103 ha100 hd110 ha101 ha200 ha102 rq01 ha103
-ha201 hw1024a rq00 hq21 rq11 hq00 ha202 rq10 hd111 hd112 hw1002p hd113 ha203 hq10 hq11 v000 v001 v010 v002
-hw2004p v003 hq20 v100 yw0004p v101 v102 v103 v011 v210 v211 v012 v013 v110 v111 v212 v213 yq00 v200 v201 v202
-v112 v113 yw1004p yw0102p yw2104p v203 yq10 yq21 yw0124a yq01 yw1104a yw2034a yw2003v yq11 yq20
+fw014v fw001a tr00 tr01 vec fq0 tr10 tr11 lq0 ra000 ra001 fw104v lq1 fq1 pm1 ra002 ra003 pm0 rd010 ra100 rd011
+rd110 ra101 rd012 rd111 rd112 rw0003p ha200 ra102 rd013 ha000 ra103 rd113 rw0034v ha201 ha001 ha002 ha003
+ha210 rw1002p rq00 rw1024v hw0004v ha202 ha010 rq01 ha203 ha011 ha012 ha013 ivec hw2004v ha100 rq10 ha101 rq11
+ha102 ha103 hq00 hw0102v hq20 hd110 hd111 hw0124a hw1024a hd112 ha211 hq01 hd113 hw1002p ha212 hq11 hq10 ha213
+hw2124v hw2102p v000 v001 v002 hq21 v003 v010 yw0004p v011 v012 v100 v013 v101 v110 v210 v102 yw0104p v103
+yw1014p v200 v111 yw1001p v112 v113 v211 yw1124p v201 v202 v212 v203 yq01 yq00 yq10 v213 yw1102a yq11 yw2001a
+yw2114v yw2014a yq20 yw2101a yq21
 """
 
 
@@ -109,8 +110,11 @@ def tile_migration_spread_revaluation_k4_kernel(
         def load_f(h):
             nc.sync.dma_start(out=f_raw[h][:], in_=factors[:, W * h : W * (h + 1)].rearrange("(p t) m -> p t m", t=T4))
 
-        def load_t():
-            nc.sync.dma_start(out=t_raw[:].bitcast(I32), in_=migr_words.rearrange("s p n -> p s n").bitcast(I32))
+        def load_t(g):
+            nc.sync.dma_start(
+                out=t_raw[:, :, 2 * W * g : 2 * W * (g + 1)].bitcast(I32),
+                in_=migr_words[:, :, 2 * W * g : 2 * W * (g + 1)].rearrange("s p n -> p s n").bitcast(I32),
+            )
 
         for n, vec in enumerate((stress, base)):
             nc.gpsimd.dma_start(
@@ -118,18 +122,16 @@ def tile_migration_spread_revaluation_k4_kernel(
                 in_=vec.rearrange("(c t e) -> t c e", t=T4, e=T4),
             )
         make_identity(nc, ident16[:])
-        load_scales(nc.scalar, ts_raw, migr_scales)
         nc.scalar.activation(out=warm[:], in_=ident[:, 0:1], func=ACT.Identity)
-        for n, name in enumerate(LOADS.split()):
-            if n == 4:
-                load_scales(nc.scalar, e_scales, expo_scales)
-            if n == 6:
-                for tile, vec in ((dur, duration), (cvx, convexity), (ntl, notional)):
-                    nc.sync.dma_start(out=tile[:], in_=vec.rearrange("(G p t) -> p G t", p=P, t=T4))
-            if name == "T":
-                load_t()
+        for name in LOADS.split():
+            if name == "Ts":
+                load_scales(nc.sync, ts_raw, migr_scales)
+            elif name == "Es":
+                load_scales(nc.sync, e_scales, expo_scales)
             else:
-                {"L": load_l, "F": load_f, "E": load_e}[name[0]](int(name[1]))
+                {"T": load_t, "L": load_l, "F": load_f, "E": load_e}[name[0]](int(name[1]))
+        for tile, vec in ((dur, duration), (cvx, convexity), (ntl, notional)):
+            nc.sync.dma_start(out=tile[:], in_=vec.rearrange("(G p t) -> p G t", p=P, t=T4))
 
         def permute_t(g):
             nc.vector.tensor_copy(
@@ -172,6 +174,8 @@ def tile_migration_spread_revaluation_k4_kernel(
             elif engine == "a":
                 nc.scalar.copy(out=out, in_=in_)
             else:
+                out = dst[:, P * q0 : P * q1, :]
+                in_ = src[:, :, P * q0 : P * q1].rearrange("p t n -> p n t")
                 nc.gpsimd.tensor_scalar(out=out, in0=in_, scalar1=1.0, scalar2=1.0, op0=ALU.mult, op1=ALU.mult)
 
         def quantize(codes, scales, woven):

@@ -22,15 +22,15 @@ W = 512
 BANKS = 8
 
 RING = {"flat": 4, "woven": 8, "y": 6, "slope": 4}
-LOADS = "L0 F0 L1 Ts F1 E0 T0 T1 E2 Es E1"
+LOADS = "L0 L1 Rw F1 F0 Es T0 E0 Ts T1 E1 E2"
 ORDER = """
-fw014v fw001a tr00 tr01 vec fq0 tr10 tr11 lq0 ra000 ra001 fw104v lq1 fq1 pm1 ra002 ra003 pm0 rd010 ra100 rd011
-rd110 ra101 rd012 rd111 rd112 rw0003p ha200 ra102 rd013 ha000 ra103 rd113 rw0034v ha201 ha001 ha002 ha003
-ha210 rw1002p rq00 rw1024v hw0004v ha202 ha010 rq01 ha203 ha011 ha012 ha013 ivec hw2004v ha100 rq10 ha101 rq11
-ha102 ha103 hq00 hw0102v hq20 hd110 hd111 hw0124a hw1024a hd112 ha211 hq01 hd113 hw1002p ha212 hq11 hq10 ha213
-hw2124v hw2102p v000 v001 v002 hq21 v003 v010 yw0004p v011 v012 v100 v013 v101 v110 v210 v102 yw0104p v103
-yw1014p v200 v111 yw1001p v112 v113 v211 yw1124p v201 v202 v212 v203 yq01 yq00 yq10 v213 yw1102a yq11 yw2001a
-yw2114v yw2014a yq20 yw2101a yq21
+tr00 fw134a vp tr01 fw103v fq1 tr10 tr11 lq0 fw024a fw002v vec ra100 lq1 ra101 ra102 fq0 pm0 ra103 ra110
+rw1002a pm1 rd010 rw1024v rd000 rd011 rd001 rd012 ra111 ha000 rd002 ra112 rq10 ra113 ha001 ivec ha010 ha011
+rd013 ha012 rw1104v ha013 rd003 ha002 hw0104v ha003 ha200 hw0004v ha201 ha202 rq01 ha210 ha211 rq00 ha212 hq01
+rq11 ha213 hq00 hw2104v ha203 hd100 hd101 hd102 hw2004a hq21 hd103 v000 v010 v001 v002 ha110 hq20 v003 v011
+v012 ha111 ha112 yw0004v ha113 hq10 yq00 v210 v013 v211 hw1124v hw1102v v200 hq11 v201 yw0104a v212 v202 v213
+yq01 v100 v110 v203 v101 yw2124v v111 v112 v113 yw2034a v102 v103 yw2003v yw2102a yw1004a yw1101a yq21 yq20
+yw1114v yq10 yq11
 """
 
 
@@ -75,8 +75,9 @@ def tile_migration_spread_revaluation_k4_kernel(
         r_scales = kept("r_scales", [P, 2, 2, W], U8)
         y_codes = kept("y_codes", [P, 3, M], U32)
         y_scales = kept("y_scales", [P, 3, M], U8)
-        rows = kept("rows", [P, 2 * P], BF16)
-        per_j = kept("per_j", [P, 2, 2 * T4], F32)
+        rows_raw = kept("rows_raw", [2, J], BF16)
+        rows = kept("rows", [P, J], BF16)
+        per_j = kept("per_j", [P, 2, 2, T4], F32)
         dur = kept("dur", [P, 3, T4], BF16)
         cvx = kept("cvx", [P, 3, T4], BF16)
         ntl = kept("ntl", [P, 3, T4], BF16)
@@ -86,9 +87,9 @@ def tile_migration_spread_revaluation_k4_kernel(
         ident16 = kept("ident16", [P, P], BF16)
         warm = kept("warm", [P, 1], F32)
 
-        nc.vector.memset(ts_raw[:].rearrange("p s n -> p (s n)").bitcast(I32), 0)
-        nc.vector.memset(rows[:], 0.0)
+        nc.gpsimd.memset(ts_raw[:].rearrange("p s n -> p (s n)").bitcast(I32), 0)
         nc.vector.memset(e_scales[:].rearrange("p s n -> p (s n)").bitcast(I32), 0)
+        nc.vector.memset(rows[:], 0.0)
         make_identity(nc, ident[:])
 
         def load_scales(queue, plane, src):
@@ -116,16 +117,14 @@ def tile_migration_spread_revaluation_k4_kernel(
                 in_=migr_words[:, :, 2 * W * g : 2 * W * (g + 1)].rearrange("s p n -> p s n").bitcast(I32),
             )
 
-        for n, vec in enumerate((stress, base)):
-            nc.gpsimd.dma_start(
-                out=rows[T4 * n : T4 * (n + 1), :].rearrange("t (c e) -> t c e", e=T4),
-                in_=vec.rearrange("(c t e) -> t c e", t=T4, e=T4),
-            )
         make_identity(nc, ident16[:])
         nc.scalar.activation(out=warm[:], in_=ident[:, 0:1], func=ACT.Identity)
         for name in LOADS.split():
             if name == "Ts":
                 load_scales(nc.sync, ts_raw, migr_scales)
+            elif name == "Rw":
+                for n, vec in enumerate((stress, base)):
+                    nc.sync.dma_start(out=rows_raw[n : n + 1, :], in_=vec.unsqueeze(0))
             elif name == "Es":
                 load_scales(nc.sync, e_scales, expo_scales)
             else:
@@ -143,11 +142,19 @@ def tile_migration_spread_revaluation_k4_kernel(
                 in_=ts_raw[:, :, W * g : W * (g + 1)].bitcast(I32).rearrange("p s (c t) -> p s t c", t=T4),
             )
 
+        def permute_vectors():
+            nc.vector.tensor_copy(
+                out=rows[0:2, :].rearrange("p (g t c e) -> p g t c e", g=2, t=T4, e=T4),
+                in_=rows_raw[:].rearrange("p (g c t e) -> p g t c e", g=2, t=T4, e=T4),
+            )
+
         def turn_vectors():
-            b = bank(BF16, 2 * P)
-            for g in range(2):
-                nc.tensor.transpose(b[:, P * g : P * (g + 1)], rows[:, P * g : P * (g + 1)], ident16[:])
-            nc.vector.tensor_copy(out=per_j[:], in_=b[:].rearrange("p (g x) -> p g x", g=2)[:, :, 0 : 2 * T4])
+            b = bank(BF16, J)
+            for n in range(2 * T4):
+                nc.tensor.transpose(b[:, P * n : P * (n + 1)], rows[:, P * n : P * (n + 1)], ident16[:])
+            nc.vector.tensor_copy(
+                out=per_j[:].rearrange("p v g t -> p v (g t)"), in_=b[:].rearrange("p (n x) -> p x n", x=P)[:, 0:2, :]
+            )
 
         def issuer_vectors():
             nc.vector.tensor_tensor(out=quad[:], in0=ntl[:], in1=cvx[:], op=ALU.mult)
@@ -217,7 +224,7 @@ def tile_migration_spread_revaluation_k4_kernel(
                 out=flat[:, t, :].rearrange("p (u q) -> p u q", u=T4),
                 in_=b[:].rearrange("p (q u) -> p u q", u=T4),
                 func=ACT.Copy,
-                scale=per_j[:, g, t : t + 1],
+                scale=per_j[:, 0, g, t : t + 1],
             )
 
         def h_dve(G, g, c):
@@ -227,8 +234,8 @@ def tile_migration_spread_revaluation_k4_kernel(
             woven = stage("h_woven", (G, g))
             nc.vector.tensor_tensor(
                 out=woven[:].rearrange("p (u q) t -> p u q t", u=T4)[:, :, 32 * c : 32 * (c + 1), :],
-                in0=b[:].rearrange("p (t q u) -> p u q t", t=T4, u=T4),
-                in1=per_j[:, g, 0:T4].unsqueeze(1).unsqueeze(1).to_broadcast([P, T4, 32, T4]),
+                in1=b[:].rearrange("p (t q u) -> p u q t", t=T4, u=T4),
+                in0=per_j[:, 0, g, :].unsqueeze(1).unsqueeze(1).to_broadcast([P, T4, 32, T4]),
                 op=ALU.mult,
             )
 
@@ -250,8 +257,8 @@ def tile_migration_spread_revaluation_k4_kernel(
             woven = stage("r_woven", (h, g))
             nc.vector.tensor_tensor(
                 out=woven[:, P * c : P * (c + 1), :],
-                in0=b[:].rearrange("p (t n) -> p n t", t=T4),
-                in1=per_j[:, g, T4 : 2 * T4].unsqueeze(1).to_broadcast([P, P, T4]),
+                in1=b[:].rearrange("p (t n) -> p n t", t=T4),
+                in0=per_j[:, 1, g, :].unsqueeze(1).to_broadcast([P, P, T4]),
                 op=ALU.add,
             )
 
@@ -259,7 +266,7 @@ def tile_migration_spread_revaluation_k4_kernel(
             b = bank(F32, W)
             r_matmul(b[:], h, g, t, 0, W)
             flat = stage("r_flat", (h, g))
-            nc.scalar.activation(out=flat[:, t, :], in_=b[:], func=ACT.Identity, bias=per_j[:, g, T4 + t : T4 + t + 1])
+            nc.scalar.activation(out=flat[:, t, :], in_=b[:], func=ACT.Identity, bias=per_j[:, 1, g, t : t + 1])
 
         def value(G, h, t):
             b = bank(F32, W)
@@ -278,7 +285,7 @@ def tile_migration_spread_revaluation_k4_kernel(
                 out=slope[:], in_=b[:], func=ACT.Identity, scale=quad[:, G, t : t + 1], bias=lin[:, G, t : t + 1]
             )
             y = stage("y", (G, h))
-            nc.vector.tensor_tensor(out=y[:, t, :], in0=b[:], in1=slope[:], op=ALU.mult)
+            nc.vector.tensor_tensor(out=y[:, t, :], in0=slope[:], in1=b[:], op=ALU.mult)
             nc.sync.dma_start(
                 out=out_0[W * G : W * (G + 1), W * h : W * (h + 1)].rearrange("(p t) m -> p t m", t=T4)[:, t, :],
                 in_=y[:, t, :],
@@ -303,6 +310,8 @@ def tile_migration_spread_revaluation_k4_kernel(
             kind, d = step[:2], [int(ch) for ch in step if ch in "0123456789"]
             if kind == "pm":
                 permute_t(d[0])
+            elif step == "vp":
+                permute_vectors()
             elif step == "vec":
                 turn_vectors()
             elif step == "ivec":

@@ -22,15 +22,15 @@ W = 512
 BANKS = 8
 
 RING = {"flat": 4, "woven": 8, "y": 6, "slope": 4}
-LOADS = "L0 L1 Rw F1 F0 Es T0 E0 Ts T1 E1 E2"
+LOADS = "L1 Rw F0 L0 F1 T0 T1 Ts E0 E2 Es E1"
 ORDER = """
-tr00 fw134a vp tr01 fw103v fq1 tr10 tr11 lq0 fw024a fw002v vec ra100 lq1 ra101 ra102 fq0 pm0 ra103 ra110
-rw1002a pm1 rd010 rw1024v rd000 rd011 rd001 rd012 ra111 ha000 rd002 ra112 rq10 ra113 ha001 ivec ha010 ha011
-rd013 ha012 rw1104v ha013 rd003 ha002 hw0104v ha003 ha200 hw0004v ha201 ha202 rq01 ha210 ha211 rq00 ha212 hq01
-rq11 ha213 hq00 hw2104v ha203 hd100 hd101 hd102 hw2004a hq21 hd103 v000 v010 v001 v002 ha110 hq20 v003 v011
-v012 ha111 ha112 yw0004v ha113 hq10 yq00 v210 v013 v211 hw1124v hw1102v v200 hq11 v201 yw0104a v212 v202 v213
-yq01 v100 v110 v203 v101 yw2124v v111 v112 v113 yw2034a v102 v103 yw2003v yw2102a yw1004a yw1101a yq21 yq20
-yw1114v yq10 yq11
+tr10 vp tr11 fw004v fq0 vec lq1 tr00 fw104v tr01 fq1 ra010 ra011 ra012 lq0 ra013 pm1 pm0 rw0101a rd000 rd110
+rd111 ra100 rd001 ra101 ra102 ra103 rd112 rd002 rd003 ha000 rd113 ha001 rw0114p rw1004v ha002 ha010 ha003
+ha011 ha012 ivec ha013 ha100 hw0101a rq01 rq00 ha101 hw0004v hw0114v ha102 hq00 ha103 hw1034a hq01 rq11 rq10
+hd110 hd111 v000 hw1003p v001 v002 v003 v010 ha210 yw0024v hq10 ha211 hd112 hd113 yw0002a ha212 yq00 hq11 v011
+ha213 v012 v013 v100 v101 v110 v102 v103 hw2104p hd200 yw0101p hd201 hd202 hd203 yw0114a yw1004a hq21 yq01
+hq20 yq10 v111 v112 v113 v210 v200 v201 v211 v202 v212 v213 yw1103p v203 yw1134a yw2134a yq11 yw2103v yw2001v
+yq21 yw2014a yq20
 """
 
 
@@ -75,8 +75,8 @@ def tile_migration_spread_revaluation_k4_kernel(
         r_scales = kept("r_scales", [P, 2, 2, W], U8)
         y_codes = kept("y_codes", [P, 3, M], U32)
         y_scales = kept("y_scales", [P, 3, M], U8)
-        rows_raw = kept("rows_raw", [2, J], BF16)
-        rows = kept("rows", [P, J], BF16)
+        rows_raw = kept("rows_raw", [4, W], BF16)
+        rows = kept("rows", [P, W], BF16)
         per_j = kept("per_j", [P, 2, 2, T4], F32)
         dur = kept("dur", [P, 3, T4], BF16)
         cvx = kept("cvx", [P, 3, T4], BF16)
@@ -124,7 +124,7 @@ def tile_migration_spread_revaluation_k4_kernel(
                 load_scales(nc.sync, ts_raw, migr_scales)
             elif name == "Rw":
                 for n, vec in enumerate((stress, base)):
-                    nc.sync.dma_start(out=rows_raw[n : n + 1, :], in_=vec.unsqueeze(0))
+                    nc.sync.dma_start(out=rows_raw[2 * n : 2 * n + 2, :], in_=vec.rearrange("(g n) -> g n", g=2))
             elif name == "Es":
                 load_scales(nc.sync, e_scales, expo_scales)
             else:
@@ -144,16 +144,16 @@ def tile_migration_spread_revaluation_k4_kernel(
 
         def permute_vectors():
             nc.vector.tensor_copy(
-                out=rows[0:2, :].rearrange("p (g t c e) -> p g t c e", g=2, t=T4, e=T4),
-                in_=rows_raw[:].rearrange("p (g c t e) -> p g t c e", g=2, t=T4, e=T4),
+                out=rows[0:4, :].rearrange("p (t c e) -> p t c e", t=T4, e=T4),
+                in_=rows_raw[:].rearrange("p (c t e) -> p t c e", t=T4, e=T4),
             )
 
         def turn_vectors():
-            b = bank(BF16, J)
-            for n in range(2 * T4):
+            b = bank(BF16, W)
+            for n in range(T4):
                 nc.tensor.transpose(b[:, P * n : P * (n + 1)], rows[:, P * n : P * (n + 1)], ident16[:])
             nc.vector.tensor_copy(
-                out=per_j[:].rearrange("p v g t -> p v (g t)"), in_=b[:].rearrange("p (n x) -> p x n", x=P)[:, 0:2, :]
+                out=per_j[:].rearrange("p v g t -> p (v g) t"), in_=b[:].rearrange("p (t x) -> p x t", x=P)[:, 0:4, :]
             )
 
         def issuer_vectors():
@@ -183,7 +183,7 @@ def tile_migration_spread_revaluation_k4_kernel(
             else:
                 out = dst[:, P * q0 : P * q1, :]
                 in_ = src[:, :, P * q0 : P * q1].rearrange("p t n -> p n t")
-                nc.gpsimd.tensor_scalar(out=out, in0=in_, scalar1=1.0, scalar2=1.0, op0=ALU.mult, op1=ALU.mult)
+                nc.gpsimd.tensor_scalar(out=out, in0=in_, scalar1=1.0, scalar2=-0.0, op0=ALU.mult, op1=ALU.add)
 
         def quantize(codes, scales, woven):
             nc.vector.quantize_mx(out=codes.bitcast(FP8X4), scales=scales, in_=woven.rearrange("p n t -> p (n t)"))
@@ -301,7 +301,8 @@ def tile_migration_spread_revaluation_k4_kernel(
             if len([x for x in finished if x == G]) == 2:
                 groups = slice(G, G + 1)
                 for Q in range(4):
-                    nc.sync.dma_start(
+                    queue = nc.scalar if len(finished) == 6 and Q >= 2 else nc.sync
+                    queue.dma_start(
                         out=out_2[groups, 4 * Q : 4 * Q + 4, :].rearrange("G r m -> r G m").bitcast(I32),
                         in_=y_scales[32 * Q : 32 * Q + 4, groups, :].bitcast(I32),
                     )

from contextlib import ExitStack

import concourse.mybir as mybir
from concourse.masks import make_identity

I, S, J, K, M = 1536, 1024, 1024, 512, 1024
FLOPS = 2 * I * S * J + 2 * J * K * M + 2 * I * J * M

F32 = mybir.dt.float32
BF16 = mybir.dt.bfloat16
I32 = mybir.dt.int32
U32 = mybir.dt.uint32
U8 = mybir.dt.uint8
FP8X4 = mybir.dt.float8_e4m3fn_x4
FP4X4 = mybir.dt.float4_e2m1fn_x4
ALU = mybir.AluOpType
ACT = mybir.ActivationFunctionType

P = 128
T4 = 4
W = 512
BANKS = 8

RING = {"flat": 4, "woven": 8, "y": 6, "slope": 4}
LOADS = "L1 Rw F0 L0 F1 T0 T1 Ts E0 E2 Es E1"
ORDER = """
tr10 vp tr11 fw004v fq0 vec lq1 tr00 fw104v tr01 fq1 ra010 ra011 ra012 lq0 ra013 pm1 pm0 rw0101a rd000 rd110
rd111 ra100 rd001 ra101 ra102 ra103 rd112 rd002 rd003 ha000 rd113 ha001 rw0114p rw1004v ha002 ha010 ha003
ha011 ha012 ivec ha013 ha100 hw0101a rq01 rq00 ha101 hw0004v hw0114v ha102 hq00 ha103 hw1034a hq01 rq11 rq10
hd110 hd111 v000 hw1003p v001 v002 v003 v010 ha210 yw0024v hq10 ha211 hd112 hd113 yw0002a ha212 yq00 hq11 v011
ha213 v012 v013 v100 v101 v110 v102 v103 hw2104p hd200 yw0101p hd201 hd202 hd203 yw0114a yw1004a hq21 yq01
hq20 yq10 v111 v112 v113 v210 v200 v201 v211 v202 v212 v213 yw1103p v203 yw1134a yw2134a yq11 yw2103v yw2001v
yq21 yw2014a yq20
"""


def tile_migration_spread_revaluation_k4_kernel(
    tc, expo_words, expo_scales, migr_words, migr_scales, stress, loadings, factors, base,
    duration, convexity, notional, out_0, out_1, out_2,
):
    nc = tc.nc
    with ExitStack() as ctx:
        keep = ctx.enter_context(tc.tile_pool(name="keep", bufs=1))
        work = ctx.enter_context(tc.tile_pool(name="work", bufs=1))
        psum = ctx.enter_context(tc.psum_pool(name="psum", bufs=1))
        ctx.enter_context(tc.manual_schedule())

        def kept(name, shape, dtype):
            return keep.tile(shape, dtype, name=name, align_bytes=64)

        tiles = {}
        finished = []
        bank_count = []

        def bank(dtype, cols):
            tag = "bank%d" % (len(bank_count) % BANKS)
            bank_count.append(0)
            return psum.tile([P, cols], dtype, name=tag, tag=tag)

        t_raw = kept("t_raw", [P, 2, 2 * J], U8)
        ts_raw = kept("ts_raw", [P, 2, J], U8)
        t_words = kept("t_words", [P, 2, 2 * J], U8)
        t_scales = kept("t_scales", [P, 2, J], U8)
        e_words = [kept("e_words%d" % G, [P, 2, W], U32) for G in range(3)]
        e_scales = kept("e_scales", [P, 2, I], U8)
        l_raw = [kept("l_raw%d" % g, [P, T4, K], BF16) for g in range(2)]
        l_codes = kept("l_codes", [P, 2, W], U32)
        l_scales = kept("l_scales", [P, 2, W], U8)
        f_raw = [kept("f_raw%d" % h, [P, T4, W], BF16) for h in range(2)]
        f_codes = kept("f_codes", [P, 2, W], U32)
        f_scales = kept("f_scales", [P, 2, W], U8)
        h_codes = kept("h_codes", [P, 3, 2, W], U32)
        h_scales = kept("h_scales", [P, 3, 2, W], U8)
        r_codes = kept("r_codes", [P, 2, 2, W], U32)
        r_scales = kept("r_scales", [P, 2, 2, W], U8)
        y_codes = kept("y_codes", [P, 3, M], U32)
        y_scales = kept("y_scales", [P, 3, M], U8)
        rows_raw = kept("rows_raw", [4, W], BF16)
        rows = kept("rows", [P, W], BF16)
        per_j = kept("per_j", [P, 2, 2, T4], F32)
        dur = kept("dur", [P, 3, T4], BF16)
        cvx = kept("cvx", [P, 3, T4], BF16)
        ntl = kept("ntl", [P, 3, T4], BF16)
        quad = kept("quad", [P, 3, T4], F32)
        lin = kept("lin", [P, 3, T4], F32)
        ident = kept("ident", [P, P], F32)
        ident16 = kept("ident16", [P, P], BF16)
        warm = kept("warm", [P, 1], F32)

        nc.gpsimd.memset(ts_raw[:].rearrange("p s n -> p (s n)").bitcast(I32), 0)
        nc.vector.memset(e_scales[:].rearrange("p s n -> p (s n)").bitcast(I32), 0)
        nc.vector.memset(rows[:], 0.0)
        make_identity(nc, ident[:])

        def load_scales(queue, plane, src):
            for Q in range(4):
                queue.dma_start(
                    out=plane[32 * Q : 32 * Q + 4].bitcast(I32),
                    in_=src[:, 4 * Q : 4 * Q + 4, :].rearrange("s r n -> r s n").bitcast(I32),
                )

        def load_e(G):
            nc.sync.dma_start(
                out=e_words[G][:].bitcast(I32),
                in_=expo_words[:, :, W * G : W * (G + 1), :].rearrange("s p n t -> p s (n t)").bitcast(I32),
            )

        def load_l(g):
            nc.sync.dma_start(out=l_raw[g][:], in_=loadings[W * g : W * (g + 1), :].rearrange("(p e) k -> p e k", e=T4))

        def load_f(h):
            nc.sync.dma_start(out=f_raw[h][:], in_=factors[:, W * h : W * (h + 1)].rearrange("(p t) m -> p t m", t=T4))

        def load_t(g):
            nc.sync.dma_start(
                out=t_raw[:, :, 2 * W * g : 2 * W * (g + 1)].bitcast(I32),
                in_=migr_words[:, :, 2 * W * g : 2 * W * (g + 1)].rearrange("s p n -> p s n").bitcast(I32),
            )

        make_identity(nc, ident16[:])
        nc.scalar.activation(out=warm[:], in_=ident[:, 0:1], func=ACT.Identity)
        for name in LOADS.split():
            if name == "Ts":
                load_scales(nc.sync, ts_raw, migr_scales)
            elif name == "Rw":
                for n, vec in enumerate((stress, base)):
                    nc.sync.dma_start(out=rows_raw[2 * n : 2 * n + 2, :], in_=vec.rearrange("(g n) -> g n", g=2))
            elif name == "Es":
                load_scales(nc.sync, e_scales, expo_scales)
            else:
                {"T": load_t, "L": load_l, "F": load_f, "E": load_e}[name[0]](int(name[1]))
        for tile, vec in ((dur, duration), (cvx, convexity), (ntl, notional)):
            nc.sync.dma_start(out=tile[:], in_=vec.rearrange("(G p t) -> p G t", p=P, t=T4))

        def permute_t(g):
            nc.vector.tensor_copy(
                out=t_words[:, :, 2 * W * g : 2 * W * (g + 1)].bitcast(I32).rearrange("p s (t c w) -> p s t c w", t=T4, w=2),
                in_=t_raw[:, :, 2 * W * g : 2 * W * (g + 1)].bitcast(I32).rearrange("p s (c t w) -> p s t c w", t=T4, w=2),
            )
            nc.vector.tensor_copy(
                out=t_scales[:, :, W * g : W * (g + 1)].bitcast(I32).rearrange("p s (t c) -> p s t c", t=T4),
                in_=ts_raw[:, :, W * g : W * (g + 1)].bitcast(I32).rearrange("p s (c t) -> p s t c", t=T4),
            )

        def permute_vectors():
            nc.vector.tensor_copy(
                out=rows[0:4, :].rearrange("p (t c e) -> p t c e", t=T4, e=T4),
                in_=rows_raw[:].rearrange("p (c t e) -> p t c e", t=T4, e=T4),
            )

        def turn_vectors():
            b = bank(BF16, W)
            for n in range(T4):
                nc.tensor.transpose(b[:, P * n : P * (n + 1)], rows[:, P * n : P * (n + 1)], ident16[:])
            nc.vector.tensor_copy(
                out=per_j[:].rearrange("p v g t -> p (v g) t"), in_=b[:].rearrange("p (t x) -> p x t", x=P)[:, 0:4, :]
            )

        def issuer_vectors():
            nc.vector.tensor_tensor(out=quad[:], in0=ntl[:], in1=cvx[:], op=ALU.mult)
            nc.vector.scalar_tensor_tensor(out=lin[:], in0=ntl[:], scalar=-1.0, in1=dur[:], op0=ALU.mult, op1=ALU.mult)

        def turn_l(g, half):
            b = bank(F32, W)
            words = l_raw[g][:].bitcast(F32)
            for x in range(2):
                for u in range(2):
                    n = 2 * x + u
                    nc.tensor.transpose(b[:, P * n : P * (n + 1)], words[:, 2 * half + x, u : K // 2 : 2], ident[:])
            dst = stage("l_woven", g)[:].rearrange("p n t -> p (n t)").bitcast(F32)
            nc.scalar.copy(
                out=dst.rearrange("p (t c h n) -> p t c h n", t=T4, h=2, n=4)[:, :, :, half, :],
                in_=b[:].rearrange("p (n c t) -> p t c n", n=4, t=T4),
            )

        def weave(engine, dst, src, q0, q1):
            out = dst[:, P * q0 : P * q1, :].rearrange("p (c i) t -> p c t i", i=4)
            in_ = src[:, :, P * q0 : P * q1].rearrange("p t (c i) -> p c t i", i=4)
            if engine == "v":
                nc.vector.tensor_copy(out=out, in_=in_)
            elif engine == "a":
                nc.scalar.copy(out=out, in_=in_)
            else:
                out = dst[:, P * q0 : P * q1, :]
                in_ = src[:, :, P * q0 : P * q1].rearrange("p t n -> p n t")
                nc.gpsimd.tensor_scalar(out=out, in0=in_, scalar1=1.0, scalar2=-0.0, op0=ALU.mult, op1=ALU.add)

        def quantize(codes, scales, woven):
            nc.vector.quantize_mx(out=codes.bitcast(FP8X4), scales=scales, in_=woven.rearrange("p n t -> p (n t)"))


        used = {"flat": 0, "woven": 0, "y": 0, "slope": 0}

        def fresh(ring, shape, dtype):
            tag = "%s%d" % (ring, used[ring] % RING[ring])
            used[ring] = used[ring] + 1
            return work.tile(shape, dtype, name=tag, tag=tag, align_bytes=64)

        def stage(kind, key):
            if (kind, key) not in tiles:
                ring = kind.split("_")[-1]
                shape = [P, W, T4] if ring == "woven" else [P, T4, W]
                tiles[(kind, key)] = fresh(ring, shape, F32 if ring == "y" else BF16)
            return tiles[(kind, key)]

        def h_matmul(out, G, g, t, n0, n1):
            col = W * g + P * t
            for s in range(2):
                nc.tensor.matmul_mx(
                    out=out,
                    lhsT=t_words[:, s, 2 * col : 2 * (col + P)].bitcast(FP4X4),
                    lhsT_scale=t_scales[:, s, col : col + P],
                    rhs=e_words[G][:, s, n0:n1].bitcast(FP8X4),
                    rhs_scale=e_scales[:, s, W * G + n0 : W * G + n1],
                    start=(s == 0),
                    stop=(s == 1),
                )

        def h_act(G, g, t):
            b = bank(F32, W)
            h_matmul(b[:], G, g, t, 0, W)
            flat = stage("h_flat", (G, g))
            nc.scalar.activation(
                out=flat[:, t, :].rearrange("p (u q) -> p u q", u=T4),
                in_=b[:].rearrange("p (q u) -> p u q", u=T4),
                func=ACT.Copy,
                scale=per_j[:, 0, g, t : t + 1],
            )

        def h_dve(G, g, c):
            b = bank(F32, W)
            for t in range(T4):
                h_matmul(b[:, P * t : P * (t + 1)], G, g, t, P * c, P * (c + 1))
            woven = stage("h_woven", (G, g))
            nc.vector.tensor_tensor(
                out=woven[:].rearrange("p (u q) t -> p u q t", u=T4)[:, :, 32 * c : 32 * (c + 1), :],
                in1=b[:].rearrange("p (t q u) -> p u q t", t=T4, u=T4),
                in0=per_j[:, 0, g, :].unsqueeze(1).unsqueeze(1).to_broadcast([P, T4, 32, T4]),
                op=ALU.mult,
            )

        def r_matmul(out, h, g, t, n0, n1):
            nc.tensor.matmul_mx(
                out=out,
                lhsT=l_codes[:, g, P * t : P * (t + 1)].bitcast(FP8X4),
                lhsT_scale=l_scales[:, g, P * t : P * (t + 1)],
                rhs=f_codes[:, h, n0:n1].bitcast(FP8X4),
                rhs_scale=f_scales[:, h, n0:n1],
                start=True,
                stop=True,
            )

        def r_dve(h, g, c):
            b = bank(F32, W)
            for t in range(T4):
                r_matmul(b[:, P * t : P * (t + 1)], h, g, t, P * c, P * (c + 1))
            woven = stage("r_woven", (h, g))
            nc.vector.tensor_tensor(
                out=woven[:, P * c : P * (c + 1), :],
                in1=b[:].rearrange("p (t n) -> p n t", t=T4),
                in0=per_j[:, 1, g, :].unsqueeze(1).to_broadcast([P, P, T4]),
                op=ALU.add,
            )

        def r_act(h, g, t):
            b = bank(F32, W)
            r_matmul(b[:], h, g, t, 0, W)
            flat = stage("r_flat", (h, g))
            nc.scalar.activation(out=flat[:, t, :], in_=b[:], func=ACT.Identity, bias=per_j[:, 1, g, t : t + 1])

        def value(G, h, t):
            b = bank(F32, W)
            for g in range(2):
                nc.tensor.matmul_mx(
                    out=b[:],
                    lhsT=h_codes[:, G, g, P * t : P * (t + 1)].bitcast(FP8X4),
                    lhsT_scale=h_scales[:, G, g, P * t : P * (t + 1)],
                    rhs=r_codes[:, h, g, :].bitcast(FP8X4),
                    rhs_scale=r_scales[:, h, g, :],
                    start=(g == 0),
                    stop=(g == 1),
                )
            slope = fresh("slope", [P, W], F32)
            nc.scalar.activation(
                out=slope[:], in_=b[:], func=ACT.Identity, scale=quad[:, G, t : t + 1], bias=lin[:, G, t : t + 1]
            )
            y = stage("y", (G, h))
            nc.vector.tensor_tensor(out=y[:, t, :], in0=slope[:], in1=b[:], op=ALU.mult)
            nc.sync.dma_start(
                out=out_0[W * G : W * (G + 1), W * h : W * (h + 1)].rearrange("(p t) m -> p t m", t=T4)[:, t, :],
                in_=y[:, t, :],
            )

        def y_planes(G, h):
            cols = slice(W * h, W * (h + 1))
            quantize(y_codes[:, G, cols], y_scales[:, G, cols], tiles[("y_woven", (G, h))][:])
            nc.sync.dma_start(
                out=out_1[G, :, cols, :].rearrange("p m t -> p (m t)").bitcast(I32), in_=y_codes[:, G, cols].bitcast(I32)
            )
            finished.append(G)
            if len([x for x in finished if x == G]) == 2:
                groups = slice(G, G + 1)
                for Q in range(4):
                    queue = nc.scalar if len(finished) == 6 and Q >= 2 else nc.sync
                    queue.dma_start(
                        out=out_2[groups, 4 * Q : 4 * Q + 4, :].rearrange("G r m -> r G m").bitcast(I32),
                        in_=y_scales[32 * Q : 32 * Q + 4, groups, :].bitcast(I32),
                    )

        for step in ORDER.split():
            kind, d = step[:2], [int(ch) for ch in step if ch in "0123456789"]
            if kind == "pm":
                permute_t(d[0])
            elif step == "vp":
                permute_vectors()
            elif step == "vec":
                turn_vectors()
            elif step == "ivec":
                issuer_vectors()
            elif kind == "tr":
                turn_l(d[0], d[1])
            elif kind == "lq":
                quantize(l_codes[:, d[0], :], l_scales[:, d[0], :], stage("l_woven", d[0])[:])
            elif kind == "fw":
                weave(step[-1], stage("f_woven", d[0]), f_raw[d[0]], d[1], d[2])
            elif kind == "fq":
                quantize(f_codes[:, d[0], :], f_scales[:, d[0], :], stage("f_woven", d[0])[:])
            elif kind == "ha":
                h_act(d[0], d[1], d[2])
            elif kind == "hd":
                h_dve(d[0], d[1], d[2])
            elif kind == "hw":
                key = (d[0], d[1])
                weave(step[-1], stage("h_woven", key), tiles[("h_flat", key)], d[2], d[3])
            elif kind == "hq":
                quantize(h_codes[:, d[0], d[1], :], h_scales[:, d[0], d[1], :], tiles[("h_woven", (d[0], d[1]))][:])
            elif kind == "rd":
                r_dve(d[0], d[1], d[2])
            elif kind == "ra":
                r_act(d[0], d[1], d[2])
            elif kind == "rw":
                key = (d[0], d[1])
                weave(step[-1], stage("r_woven", key), tiles[("r_flat", key)], d[2], d[3])
            elif kind == "rq":
                quantize(r_codes[:, d[0], d[1], :], r_scales[:, d[0], d[1], :], tiles[("r_woven", (d[0], d[1]))][:])
            elif kind == "yw":
                key = (d[0], d[1])
                weave(step[-1], stage("y_woven", key), tiles[("y", key)], d[2], d[3])
            elif kind == "yq":
                y_planes(d[0], d[1])
            else:
                value(d[0], d[1], d[2])
